import numpy as np
import ml_dtypes


def mxq(x, axis, fmt="e4m3"):
    dtype, down = {"e4m3": (ml_dtypes.float8_e4m3fn, 7), "e5m2": (ml_dtypes.float8_e5m2, 14)}[fmt]
    v = np.moveaxis(np.asarray(x, np.float32).astype(ml_dtypes.bfloat16).astype(np.float64), axis, -1)
    blocks = v.reshape(v.shape[:-1] + (-1, 32))
    amax = np.abs(blocks).max(-1, keepdims=True)
    byte = np.maximum(np.where(amax > 0, np.frexp(amax)[1] - 1 + 127, 0) - down, 1)
    scale = np.exp2(byte - 127.0)
    codes = (blocks / scale).astype(np.float32).astype(dtype).astype(np.float64)
    return np.moveaxis((codes * scale).reshape(v.shape), -1, axis)


WIDE = False


def mx_kscale(k, group=512):
    if not WIDE:
        return np.ones(k)
    levels = np.array([18, -18])
    if group != 512:
        return np.exp2(np.random.permutation(np.resize(levels, k // group))).repeat(group)
    if k % 512:
        return np.exp2(np.random.permutation(np.resize(levels, k // 32))).repeat(32)
    a = np.empty((k // 512, 16))
    for p in range(k // 512):
        a[p, :8] = np.random.permutation(np.resize(levels, 8))
        for g in range(8):
            far = levels[np.abs(levels - a[p, g]) >= 10]
            a[p, g + 8] = far[np.random.randint(len(far))]
    return np.exp2(a.ravel()).repeat(32)


def f64(x):
    return np.asarray(x).astype(np.float64)


def sigmoid(v):
    return 1.0 / (1.0 + np.exp(-v))


G, D, M, O, N = 4, 128, 128, 128, 512


def setup_inputs():
    n = np.random.standard_normal
    s_d = mx_kscale(D, 0)
    s_o = mx_kscale(O, 0)
    return {
        "x": (n((G, D, N)) * s_d[:, None]).astype(np.float32),
        "w1": (n((G, D, M)) / np.sqrt(D) / s_d[:, None]).astype(np.float32),
        "w2": (n((G, D, M)) / np.sqrt(D) / s_d[:, None]).astype(np.float32),
        "tp": (np.random.uniform(0.5, 1.2, (G, M, 1))).astype(np.float32),
        "wo": (n((G, O, M)) / np.sqrt(O) / s_o[:, None]).astype(np.float32),
        "dy": (n((G, O, N)) * s_o[:, None]).astype(np.float32),
        "old": (0.3 * n((G, M, N))).astype(np.float32),
    }


def reference(x, w1, w2, tp, wo, dy, old):
    w1q = mxq(f64(w1), 1, "e4m3")
    xq = mxq(f64(x), 1, "e4m3")
    z1 = w1q.transpose(0, 2, 1) @ xq
    w2q = mxq(f64(w2), 1, "e4m3")
    z2 = w2q.transpose(0, 2, 1) @ xq
    s1 = z1 * f64(tp)
    woq = mxq(f64(wo), 1, "e4m3")
    dyq = mxq(f64(dy), 1, "e4m3")
    c0 = woq.transpose(0, 2, 1) @ dyq
    dls = np.sum(c0 * sigmoid(z2) * (-1.0), axis=-1, keepdims=True)
    ds1 = c0 * sigmoid(z2) + dls / np.sum(np.exp(s1), axis=-1, keepdims=True) * np.exp(s1)
    dz1 = ds1 * f64(tp)
    y = dz1 + f64(old)
    return y

@@ -1,0 +1,168 @@
+from contextlib import ExitStack
+
+import concourse.mybir as mybir
+
+G, D, M, N = 4, 128, 128, 512
+FLOPS = 3 * 2 * G * D * M * N
+
+F32 = mybir.dt.float32
+BF16 = mybir.dt.bfloat16
+U32 = mybir.dt.uint32
+U8 = mybir.dt.uint8
+FP8X4 = mybir.dt.float8_e4m3fn_x4
+ACT = mybir.ActivationFunctionType
+ALU = mybir.AluOpType
+
+P = 128
+PACK = 4
+ROWS = D // PACK
+HALF = N // 2
+X_SPLIT = 336
+DY_SPLIT = 176
+
+
+def packed_rows(t):
+    return t.rearrange("g (p j) c -> (g p) j c", j=PACK)
+
+
+def interleave(copy, dst, src):
+    copy(
+        out=dst.rearrange("p (c i) j -> p c j i", i=4),
+        in_=src.rearrange("p j (c i) -> p c j i", i=4),
+    )
+
+
+def quantize(nc, codes, scales, src):
+    nc.vector.quantize_mx(out=codes.bitcast(FP8X4), scales=scales, in_=src.rearrange("p c j -> p (c j)"))
+
+
+def tile_rows_browlog_kernel(tc, x, w1, w2, tp, wo, dy, old, out):
+    nc = tc.nc
+    with ExitStack() as ctx:
+        sb = ctx.enter_context(tc.tile_pool(name="sb", bufs=1))
+        ps = ctx.enter_context(tc.psum_pool(name="ps", bufs=1))
+        ctx.enter_context(tc.manual_schedule())
+
+        w2_raw = sb.tile([P, PACK, M], F32, name="w2_raw")
+        wo_raw = sb.tile([P, PACK, M], F32, name="wo_raw")
+        w1_raw = sb.tile([P, PACK, M], F32, name="w1_raw")
+        x_raw = sb.tile([P, PACK, N], F32, name="x_raw")
+        dy_raw = [sb.tile([P, PACK, HALF], F32, name="dy_raw%d" % h) for h in range(2)]
+        tp_sb = sb.tile([P, G], F32, name="tp_sb")
+        old_sb = [sb.tile([P, 2, N], F32, name="old%d" % h) for h in range(2)]
+
+        nc.sync.dma_start(out=w2_raw[:], in_=packed_rows(w2))
+        nc.sync.dma_start(out=wo_raw[:], in_=packed_rows(wo))
+        nc.sync.dma_start(out=x_raw[:], in_=packed_rows(x))
+        for h in range(2):
+            nc.sync.dma_start(out=dy_raw[h][:], in_=packed_rows(dy)[:, :, h * HALF : (h + 1) * HALF])
+        nc.sync.dma_start(out=w1_raw[:], in_=packed_rows(w1))
+        with nc.allow_non_contiguous_dma(reason="one temper a partition and group"):
+            nc.sync.dma_start(out=tp_sb[:], in_=tp.rearrange("g m o -> m (g o)"))
+        for h in range(2):
+            nc.sync.dma_start(out=old_sb[h][:], in_=old[2 * h : 2 * h + 2].rearrange("g m n -> m g n"))
+
+        def operand(name, cols):
+            return (
+                sb.tile([P, cols, PACK], BF16, name=name + "_bf", align_bytes=64),
+                sb.tile([P, cols], U32, name=name + "_codes", align_bytes=64),
+                sb.tile([P, cols], U8, name=name + "_scales", align_bytes=64),
+            )
+
+        w2_bf, w2_codes, w2_scales = operand("w2", M)
+        wo_bf, wo_codes, wo_scales = operand("wo", M)
+        w1_bf, w1_codes, w1_scales = operand("w1", M)
+        x_bf, x_codes, x_scales = operand("x", N)
+        dy_bf, dy_codes, dy_scales = operand("dy", N)
+
+        z_bank = [ps.tile([M, N], F32, name="z_bank%d" % g) for g in range(G)]
+        c_bank = [ps.tile([M, N], F32, name="c_bank%d" % g) for g in range(G)]
+
+        def products(banks, w_codes, w_scales, a_codes, a_scales):
+            for g in range(G):
+                rows = slice(ROWS * g, ROWS * (g + 1))
+                nc.tensor.matmul_mx(
+                    out=banks[g][:],
+                    lhsT=w_codes[rows, :].bitcast(FP8X4),
+                    lhsT_scale=w_scales[rows, :],
+                    rhs=a_codes[rows, :].bitcast(FP8X4),
+                    rhs_scale=a_scales[rows, :],
+                    start=True,
+                    stop=True,
+                )
+
+        th = [sb.tile([M, N], F32, name="th%d" % g) for g in range(G)]
+        ex = [sb.tile([M, N], F32, name="ex%d" % g) for g in range(G)]
+        u = [sb.tile([M, N], F32, name="u%d" % g) for g in range(G)]
+        v = [sb.tile([M, N], F32, name="v%d" % g) for g in range(G)]
+        res = [sb.tile([M, N], F32, name="res%d" % g) for g in range(G)]
+        ex_sum = sb.tile([M, G], F32, name="ex_sum")
+        u_sum = sb.tile([M, G], F32, name="u_sum")
+        half_tp = sb.tile([M, G], F32, name="half_tp")
+        inv_sum = sb.tile([M, G], F32, name="inv_sum")
+        lead = sb.tile([M, G], F32, name="lead")
+        k = sb.tile([M, G], F32, name="k")
+
+        interleave(nc.vector.tensor_copy, w2_bf[:], w2_raw[:])
+        interleave(nc.vector.tensor_copy, wo_bf[:], wo_raw[:])
+        quantize(nc, w2_codes[:], w2_scales[:], w2_bf[:])
+        quantize(nc, wo_codes[:], wo_scales[:], wo_bf[:])
+
+        interleave(nc.vector.tensor_copy, x_bf[:, :X_SPLIT, :], x_raw[:, :, :X_SPLIT])
+        interleave(nc.scalar.copy, x_bf[:, X_SPLIT:, :], x_raw[:, :, X_SPLIT:])
+        quantize(nc, x_codes[:], x_scales[:], x_bf[:])
+        products(z_bank, w2_codes, w2_scales, x_codes, x_scales)
+
+        def tanh(g):
+            nc.scalar.activation(out=th[g][:], in_=z_bank[g][:], func=ACT.Tanh, scale=0.5)
+
+        tanh(0)
+        interleave(nc.vector.tensor_copy, dy_bf[:, :HALF, :], dy_raw[0][:])
+        interleave(nc.vector.tensor_copy, dy_bf[:, HALF : HALF + DY_SPLIT, :], dy_raw[1][:, :, :DY_SPLIT])
+        interleave(nc.scalar.copy, dy_bf[:, HALF + DY_SPLIT :, :], dy_raw[1][:, :, DY_SPLIT:])
+        for h in range(2):
+            cols = slice(h * HALF, (h + 1) * HALF)
+            quantize(nc, dy_codes[:, cols], dy_scales[:, cols], dy_bf[:, cols, :])
+        products(c_bank, wo_codes, wo_scales, dy_codes, dy_scales)
+        for g in range(1, G):
+            tanh(g)
+
+        interleave(nc.vector.tensor_copy, w1_bf[:], w1_raw[:])
+        nc.vector.tensor_scalar(out=half_tp[:], in0=tp_sb[:], scalar1=0.5, scalar2=None, op0=ALU.mult)
+        quantize(nc, w1_codes[:], w1_scales[:], w1_bf[:])
+        products(z_bank, w1_codes, w1_scales, x_codes, x_scales)
+        for g in range(G):
+            nc.scalar.activation(
+                out=ex[g][:], in_=z_bank[g][:], func=ACT.Exp, scale=tp_sb[:, g : g + 1], accum_out=ex_sum[:, g : g + 1]
+            )
+
+        for g in range(G):
+            nc.vector.scalar_tensor_tensor(
+                out=u[g][:], in0=th[g][:], scalar=1.0, in1=c_bank[g][:], op0=ALU.add, op1=ALU.mult,
+                accum_out=u_sum[:, g : g + 1],
+            )
+
+        def with_old(g):
+            nc.vector.scalar_tensor_tensor(
+                out=v[g][:], in0=u[g][:], scalar=half_tp[:, g : g + 1], in1=old_sb[g // 2][:, g % 2, :],
+                op0=ALU.mult, op1=ALU.add,
+            )
+
+        def finish(g):
+            nc.vector.scalar_tensor_tensor(
+                out=res[g][:], in0=ex[g][:], scalar=k[:, g : g + 1], in1=v[g][:], op0=ALU.mult, op1=ALU.add
+            )
+            nc.sync.dma_start(out=out[g], in_=res[g][:])
+
+        with_old(0)
+        nc.vector.scalar_tensor_tensor(
+            out=lead[:], in0=u_sum[:], scalar=-1.0, in1=half_tp[:], op0=ALU.mult, op1=ALU.mult
+        )
+        nc.vector.reciprocal(out=inv_sum[:], in_=ex_sum[:])
+        with_old(1)
+        nc.vector.tensor_tensor(out=k[:], in0=lead[:], in1=inv_sum[:], op=ALU.mult)
+        with_old(2)
+        finish(0)
+        with_old(3)
+        for g in range(1, G):
+            finish(g)

@@ -51,11 +51,11 @@ def tile_rows_browlog_kernel(tc, x, w1, w2, tp, wo, dy, old, out):
         tp_sb = sb.tile([P, G], F32, name="tp_sb")
         old_sb = [sb.tile([P, 2, N], F32, name="old%d" % h) for h in range(2)]
 
-        nc.sync.dma_start(out=w2_raw[:], in_=packed_rows(w2))
-        nc.sync.dma_start(out=wo_raw[:], in_=packed_rows(wo))
         nc.sync.dma_start(out=x_raw[:], in_=packed_rows(x))
-        for h in range(2):
-            nc.sync.dma_start(out=dy_raw[h][:], in_=packed_rows(dy)[:, :, h * HALF : (h + 1) * HALF])
+        nc.sync.dma_start(out=w2_raw[:], in_=packed_rows(w2))
+        nc.sync.dma_start(out=dy_raw[0][:], in_=packed_rows(dy)[:, :, :HALF])
+        nc.sync.dma_start(out=wo_raw[:], in_=packed_rows(wo))
+        nc.sync.dma_start(out=dy_raw[1][:], in_=packed_rows(dy)[:, :, HALF:])
         nc.sync.dma_start(out=w1_raw[:], in_=packed_rows(w1))
         with nc.allow_non_contiguous_dma(reason="one temper a partition and group"):
             nc.sync.dma_start(out=tp_sb[:], in_=tp.rearrange("g m o -> m (g o)"))
@@ -103,26 +103,24 @@ def tile_rows_browlog_kernel(tc, x, w1, w2, tp, wo, dy, old, out):
         lead = sb.tile([M, G], F32, name="lead")
         k = sb.tile([M, G], F32, name="k")
 
-        interleave(nc.vector.tensor_copy, w2_bf[:], w2_raw[:])
-        interleave(nc.vector.tensor_copy, wo_bf[:], wo_raw[:])
-        quantize(nc, w2_codes[:], w2_scales[:], w2_bf[:])
-        quantize(nc, wo_codes[:], wo_scales[:], wo_bf[:])
-
         interleave(nc.vector.tensor_copy, x_bf[:, :X_SPLIT, :], x_raw[:, :, :X_SPLIT])
         interleave(nc.scalar.copy, x_bf[:, X_SPLIT:, :], x_raw[:, :, X_SPLIT:])
+        interleave(nc.scalar.copy, w2_bf[:], w2_raw[:])
         quantize(nc, x_codes[:], x_scales[:], x_bf[:])
+        quantize(nc, w2_codes[:], w2_scales[:], w2_bf[:])
         products(z_bank, w2_codes, w2_scales, x_codes, x_scales)
 
         def tanh(g):
             nc.scalar.activation(out=th[g][:], in_=z_bank[g][:], func=ACT.Tanh, scale=0.5)
 
-        tanh(0)
         interleave(nc.vector.tensor_copy, dy_bf[:, :HALF, :], dy_raw[0][:])
+        interleave(nc.scalar.copy, wo_bf[:], wo_raw[:])
+        quantize(nc, dy_codes[:, :HALF], dy_scales[:, :HALF], dy_bf[:, :HALF, :])
+        quantize(nc, wo_codes[:], wo_scales[:], wo_bf[:])
+        tanh(0)
         interleave(nc.vector.tensor_copy, dy_bf[:, HALF : HALF + DY_SPLIT, :], dy_raw[1][:, :, :DY_SPLIT])
         interleave(nc.scalar.copy, dy_bf[:, HALF + DY_SPLIT :, :], dy_raw[1][:, :, DY_SPLIT:])
-        for h in range(2):
-            cols = slice(h * HALF, (h + 1) * HALF)
-            quantize(nc, dy_codes[:, cols], dy_scales[:, cols], dy_bf[:, cols, :])
+        quantize(nc, dy_codes[:, HALF:], dy_scales[:, HALF:], dy_bf[:, HALF:, :])
         products(c_bank, wo_codes, wo_scales, dy_codes, dy_scales)
         for g in range(1, G):
             tanh(g)
@@ -158,11 +156,14 @@ def tile_rows_browlog_kernel(tc, x, w1, w2, tp, wo, dy, old, out):
         nc.vector.scalar_tensor_tensor(
             out=lead[:], in0=u_sum[:], scalar=-1.0, in1=half_tp[:], op0=ALU.mult, op1=ALU.mult
         )
-        nc.vector.reciprocal(out=inv_sum[:], in_=ex_sum[:])
         with_old(1)
-        nc.vector.tensor_tensor(out=k[:], in0=lead[:], in1=inv_sum[:], op=ALU.mult)
+        nc.vector.reciprocal(out=inv_sum[:, 0:2], in_=ex_sum[:, 0:2])
         with_old(2)
-        finish(0)
+        nc.vector.tensor_tensor(out=k[:, 0:2], in0=lead[:, 0:2], in1=inv_sum[:, 0:2], op=ALU.mult)
         with_old(3)
-        for g in range(1, G):
-            finish(g)
+        finish(0)
+        nc.vector.reciprocal(out=inv_sum[:, 2:4], in_=ex_sum[:, 2:4])
+        finish(1)
+        nc.vector.tensor_tensor(out=k[:, 2:4], in0=lead[:, 2:4], in1=inv_sum[:, 2:4], op=ALU.mult)
+        finish(2)
+        finish(3)

@@ -16,19 +16,22 @@ ALU = mybir.AluOpType
 P = 128
 PACK = 4
 ROWS = D // PACK
+SQUARE = 32
+RUN = 4
 HALF = N // 2
-X_SPLIT = 336
-DY_SPLIT = 176
+
+X_VECTOR_COLS = 336
+DY_VECTOR_COLS = 176
 
 
 def packed_rows(t):
     return t.rearrange("g (p j) c -> (g p) j c", j=PACK)
 
 
-def interleave(copy, dst, src):
+def round_and_interleave(copy, dst, src):
     copy(
-        out=dst.rearrange("p (c i) j -> p c j i", i=4),
-        in_=src.rearrange("p j (c i) -> p c j i", i=4),
+        out=dst.rearrange("p (c i) j -> p c j i", i=RUN),
+        in_=src.rearrange("p j (c i) -> p c j i", i=RUN),
     )
 
 
@@ -43,24 +46,28 @@ def tile_rows_browlog_kernel(tc, x, w1, w2, tp, wo, dy, old, out):
         ps = ctx.enter_context(tc.psum_pool(name="ps", bufs=1))
         ctx.enter_context(tc.manual_schedule())
 
+        x_raw = sb.tile([P, PACK, N], F32, name="x_raw")
         w2_raw = sb.tile([P, PACK, M], F32, name="w2_raw")
         wo_raw = sb.tile([P, PACK, M], F32, name="wo_raw")
         w1_raw = sb.tile([P, PACK, M], F32, name="w1_raw")
-        x_raw = sb.tile([P, PACK, N], F32, name="x_raw")
         dy_raw = [sb.tile([P, PACK, HALF], F32, name="dy_raw%d" % h) for h in range(2)]
-        tp_sb = sb.tile([P, G], F32, name="tp_sb")
-        old_sb = [sb.tile([P, 2, N], F32, name="old%d" % h) for h in range(2)]
+        old_sb = [sb.tile([M, N], F32, name="old%d" % g) for g in range(G)]
+        tp_rows = sb.tile([P, G * SQUARE], F32, name="tp_rows", align_bytes=64)
+        tp_cols = sb.tile([P, G * SQUARE], F32, name="tp_cols", align_bytes=64)
 
+        nc.vector.memset(tp_rows[:], 0.0)
         nc.sync.dma_start(out=x_raw[:], in_=packed_rows(x))
+        nc.sync.dma_start(
+            out=tp_rows[0:P:SQUARE, :].rearrange("b (g c) -> b g c", c=SQUARE),
+            in_=tp.rearrange("g (b c) o -> b g (c o)", c=SQUARE),
+        )
         nc.sync.dma_start(out=w2_raw[:], in_=packed_rows(w2))
         nc.sync.dma_start(out=dy_raw[0][:], in_=packed_rows(dy)[:, :, :HALF])
         nc.sync.dma_start(out=wo_raw[:], in_=packed_rows(wo))
         nc.sync.dma_start(out=dy_raw[1][:], in_=packed_rows(dy)[:, :, HALF:])
         nc.sync.dma_start(out=w1_raw[:], in_=packed_rows(w1))
-        with nc.allow_non_contiguous_dma(reason="one temper a partition and group"):
-            nc.sync.dma_start(out=tp_sb[:], in_=tp.rearrange("g m o -> m (g o)"))
-        for h in range(2):
-            nc.sync.dma_start(out=old_sb[h][:], in_=old[2 * h : 2 * h + 2].rearrange("g m n -> m g n"))
+        for g in range(G):
+            nc.sync.dma_start(out=old_sb[g][:], in_=old[g])
 
         def operand(name, cols):
             return (
@@ -69,11 +76,11 @@ def tile_rows_browlog_kernel(tc, x, w1, w2, tp, wo, dy, old, out):
                 sb.tile([P, cols], U8, name=name + "_scales", align_bytes=64),
             )
 
+        x_bf, x_codes, x_scales = operand("x", N)
         w2_bf, w2_codes, w2_scales = operand("w2", M)
+        dy_bf, dy_codes, dy_scales = operand("dy", N)
         wo_bf, wo_codes, wo_scales = operand("wo", M)
         w1_bf, w1_codes, w1_scales = operand("w1", M)
-        x_bf, x_codes, x_scales = operand("x", N)
-        dy_bf, dy_codes, dy_scales = operand("dy", N)
 
         z_bank = [ps.tile([M, N], F32, name="z_bank%d" % g) for g in range(G)]
         c_bank = [ps.tile([M, N], F32, name="c_bank%d" % g) for g in range(G)]
@@ -92,78 +99,124 @@ def tile_rows_browlog_kernel(tc, x, w1, w2, tp, wo, dy, old, out):
                 )
 
         th = [sb.tile([M, N], F32, name="th%d" % g) for g in range(G)]
+        gate0 = sb.tile([M, N], F32, name="gate0")
         ex = [sb.tile([M, N], F32, name="ex%d" % g) for g in range(G)]
-        u = [sb.tile([M, N], F32, name="u%d" % g) for g in range(G)]
-        v = [sb.tile([M, N], F32, name="v%d" % g) for g in range(G)]
+        prod = [sb.tile([M, N], F32, name="prod%d" % g) for g in range(G)]
+        part = [sb.tile([M, N], F32, name="part%d" % g) for g in range(G)]
         res = [sb.tile([M, N], F32, name="res%d" % g) for g in range(G)]
         ex_sum = sb.tile([M, G], F32, name="ex_sum")
-        u_sum = sb.tile([M, G], F32, name="u_sum")
+        prod_sum = sb.tile([M, G], F32, name="prod_sum")
+        inv_ex_sum = sb.tile([M, G], F32, name="inv_ex_sum")
         half_tp = sb.tile([M, G], F32, name="half_tp")
-        inv_sum = sb.tile([M, G], F32, name="inv_sum")
-        lead = sb.tile([M, G], F32, name="lead")
-        k = sb.tile([M, G], F32, name="k")
-
-        interleave(nc.vector.tensor_copy, x_bf[:, :X_SPLIT, :], x_raw[:, :, :X_SPLIT])
-        interleave(nc.scalar.copy, x_bf[:, X_SPLIT:, :], x_raw[:, :, X_SPLIT:])
-        interleave(nc.scalar.copy, w2_bf[:], w2_raw[:])
-        quantize(nc, x_codes[:], x_scales[:], x_bf[:])
-        quantize(nc, w2_codes[:], w2_scales[:], w2_bf[:])
-        products(z_bank, w2_codes, w2_scales, x_codes, x_scales)
+        minus_half_tp = sb.tile([M, G], F32, name="minus_half_tp")
+        factor = sb.tile([M, G], F32, name="factor")
+        tp_of_groups = tp_cols[:, 0 : G * SQUARE : SQUARE]
 
         def tanh(g):
             nc.scalar.activation(out=th[g][:], in_=z_bank[g][:], func=ACT.Tanh, scale=0.5)
 
-        interleave(nc.vector.tensor_copy, dy_bf[:, :HALF, :], dy_raw[0][:])
-        interleave(nc.scalar.copy, wo_bf[:], wo_raw[:])
+        round_and_interleave(nc.vector.tensor_copy, x_bf[:, :X_VECTOR_COLS, :], x_raw[:, :, :X_VECTOR_COLS])
+        round_and_interleave(nc.scalar.copy, x_bf[:, X_VECTOR_COLS:, :], x_raw[:, :, X_VECTOR_COLS:])
+        round_and_interleave(nc.scalar.copy, w2_bf[:], w2_raw[:])
+        nc.vector.transpose(out=tp_cols[:], in_=tp_rows[:])
+        quantize(nc, x_codes[:], x_scales[:], x_bf[:])
+        quantize(nc, w2_codes[:], w2_scales[:], w2_bf[:])
+        nc.vector.tensor_scalar(out=half_tp[:], in0=tp_of_groups, scalar1=0.5, scalar2=None, op0=ALU.mult)
+        products(z_bank, w2_codes, w2_scales, x_codes, x_scales)
+
+        round_and_interleave(nc.vector.tensor_copy, dy_bf[:, :HALF, :], dy_raw[0][:])
+        round_and_interleave(nc.scalar.copy, wo_bf[:], wo_raw[:])
         quantize(nc, dy_codes[:, :HALF], dy_scales[:, :HALF], dy_bf[:, :HALF, :])
         quantize(nc, wo_codes[:], wo_scales[:], wo_bf[:])
         tanh(0)
-        interleave(nc.vector.tensor_copy, dy_bf[:, HALF : HALF + DY_SPLIT, :], dy_raw[1][:, :, :DY_SPLIT])
-        interleave(nc.scalar.copy, dy_bf[:, HALF + DY_SPLIT :, :], dy_raw[1][:, :, DY_SPLIT:])
+        cut = HALF + DY_VECTOR_COLS
+        round_and_interleave(nc.vector.tensor_copy, dy_bf[:, HALF:cut, :], dy_raw[1][:, :, :DY_VECTOR_COLS])
+        round_and_interleave(nc.scalar.copy, dy_bf[:, cut:, :], dy_raw[1][:, :, DY_VECTOR_COLS:])
         quantize(nc, dy_codes[:, HALF:], dy_scales[:, HALF:], dy_bf[:, HALF:, :])
         products(c_bank, wo_codes, wo_scales, dy_codes, dy_scales)
+
+        nc.scalar.activation(
+            out=gate0[:], in_=th[0][:], func=ACT.Identity, scale=half_tp[:, 0:1], bias=half_tp[:, 0:1]
+        )
         for g in range(1, G):
             tanh(g)
 
-        interleave(nc.vector.tensor_copy, w1_bf[:], w1_raw[:])
-        nc.vector.tensor_scalar(out=half_tp[:], in0=tp_sb[:], scalar1=0.5, scalar2=None, op0=ALU.mult)
+        round_and_interleave(nc.vector.tensor_copy, w1_bf[:], w1_raw[:])
+        nc.vector.tensor_scalar(out=minus_half_tp[:], in0=tp_of_groups, scalar1=-0.5, scalar2=None, op0=ALU.mult)
         quantize(nc, w1_codes[:], w1_scales[:], w1_bf[:])
         products(z_bank, w1_codes, w1_scales, x_codes, x_scales)
         for g in range(G):
             nc.scalar.activation(
-                out=ex[g][:], in_=z_bank[g][:], func=ACT.Exp, scale=tp_sb[:, g : g + 1], accum_out=ex_sum[:, g : g + 1]
+                out=ex[g][:],
+                in_=z_bank[g][:],
+                func=ACT.Exp,
+                scale=tp_cols[:, SQUARE * g : SQUARE * g + 1],
+                accum_out=ex_sum[:, g : g + 1],
             )
 
-        for g in range(G):
+        def product_with_c0(g):
             nc.vector.scalar_tensor_tensor(
-                out=u[g][:], in0=th[g][:], scalar=1.0, in1=c_bank[g][:], op0=ALU.add, op1=ALU.mult,
-                accum_out=u_sum[:, g : g + 1],
+                out=prod[g][:],
+                in0=gate0[:] if g == 0 else th[g][:],
+                scalar=0.0 if g == 0 else 1.0,
+                in1=c_bank[g][:],
+                op0=ALU.add,
+                op1=ALU.mult,
+                accum_out=prod_sum[:, g : g + 1],
             )
 
-        def with_old(g):
+        def add_old(g, cols):
             nc.vector.scalar_tensor_tensor(
-                out=v[g][:], in0=u[g][:], scalar=half_tp[:, g : g + 1], in1=old_sb[g // 2][:, g % 2, :],
-                op0=ALU.mult, op1=ALU.add,
+                out=part[g][:, cols],
+                in0=prod[g][:, cols],
+                scalar=half_tp[:, g : g + 1],
+                in1=old_sb[g][:, cols],
+                op0=ALU.mult,
+                op1=ALU.add,
             )
 
-        def finish(g):
+        def invert_sums(groups):
+            nc.vector.reciprocal(out=inv_ex_sum[:, groups], in_=ex_sum[:, groups])
+
+        def row_factor(g):
+            nc.vector.tensor_scalar(
+                out=factor[:, g : g + 1],
+                in0=prod_sum[:, g : g + 1],
+                scalar1=inv_ex_sum[:, g : g + 1],
+                scalar2=-1.0 if g == 0 else minus_half_tp[:, g : g + 1],
+                op0=ALU.mult,
+                op1=ALU.mult,
+            )
+
+        def finish(g, cols):
             nc.vector.scalar_tensor_tensor(
-                out=res[g][:], in0=ex[g][:], scalar=k[:, g : g + 1], in1=v[g][:], op0=ALU.mult, op1=ALU.add
+                out=res[g][:, cols],
+                in0=ex[g][:, cols],
+                scalar=factor[:, g : g + 1],
+                in1=part[g][:, cols],
+                op0=ALU.mult,
+                op1=ALU.add,
             )
-            nc.sync.dma_start(out=out[g], in_=res[g][:])
+            nc.sync.dma_start(out=out[g][:, cols], in_=res[g][:, cols])
 
-        with_old(0)
-        nc.vector.scalar_tensor_tensor(
-            out=lead[:], in0=u_sum[:], scalar=-1.0, in1=half_tp[:], op0=ALU.mult, op1=ALU.mult
-        )
-        with_old(1)
-        nc.vector.reciprocal(out=inv_sum[:, 0:2], in_=ex_sum[:, 0:2])
-        with_old(2)
-        nc.vector.tensor_tensor(out=k[:, 0:2], in0=lead[:, 0:2], in1=inv_sum[:, 0:2], op=ALU.mult)
-        with_old(3)
-        finish(0)
-        nc.vector.reciprocal(out=inv_sum[:, 2:4], in_=ex_sum[:, 2:4])
-        finish(1)
-        nc.vector.tensor_tensor(out=k[:, 2:4], in0=lead[:, 2:4], in1=inv_sum[:, 2:4], op=ALU.mult)
-        finish(2)
-        finish(3)
+        product_with_c0(0)
+        nc.gpsimd.tensor_tensor(out=part[0][:], in0=prod[0][:], in1=old_sb[0][:], op=ALU.add)
+        for g in range(1, G):
+            product_with_c0(g)
+
+        whole, left, right = slice(0, N), slice(0, HALF), slice(HALF, N)
+        invert_sums(slice(0, 2))
+        add_old(1, whole)
+        row_factor(0)
+        row_factor(1)
+        add_old(2, whole)
+        finish(0, whole)
+        invert_sums(slice(2, 4))
+        finish(1, whole)
+        row_factor(2)
+        row_factor(3)
+        add_old(3, left)
+        finish(2, whole)
+        add_old(3, right)
+        finish(3, left)
+        finish(3, right)

from contextlib import ExitStack

import concourse.mybir as mybir

G, D, M, N = 4, 128, 128, 512
FLOPS = 3 * 2 * G * D * M * N

F32 = mybir.dt.float32
BF16 = mybir.dt.bfloat16
U32 = mybir.dt.uint32
U8 = mybir.dt.uint8
FP8X4 = mybir.dt.float8_e4m3fn_x4
ACT = mybir.ActivationFunctionType
ALU = mybir.AluOpType

P = 128
PACK = 4
ROWS = D // PACK
SQUARE = 32
RUN = 4
HALF = N // 2

X_VECTOR_COLS = 336
DY_VECTOR_COLS = 176


def packed_rows(t):
    return t.rearrange("g (p j) c -> (g p) j c", j=PACK)


def round_and_interleave(copy, dst, src):
    copy(
        out=dst.rearrange("p (c i) j -> p c j i", i=RUN),
        in_=src.rearrange("p j (c i) -> p c j i", i=RUN),
    )


def quantize(nc, codes, scales, src):
    nc.vector.quantize_mx(out=codes.bitcast(FP8X4), scales=scales, in_=src.rearrange("p c j -> p (c j)"))


def tile_rows_browlog_kernel(tc, x, w1, w2, tp, wo, dy, old, out):
    nc = tc.nc
    with ExitStack() as ctx:
        sb = ctx.enter_context(tc.tile_pool(name="sb", bufs=1))
        ps = ctx.enter_context(tc.psum_pool(name="ps", bufs=1))
        ctx.enter_context(tc.manual_schedule())

        x_raw = sb.tile([P, PACK, N], F32, name="x_raw")
        w2_raw = sb.tile([P, PACK, M], F32, name="w2_raw")
        wo_raw = sb.tile([P, PACK, M], F32, name="wo_raw")
        w1_raw = sb.tile([P, PACK, M], F32, name="w1_raw")
        dy_raw = [sb.tile([P, PACK, HALF], F32, name="dy_raw%d" % h) for h in range(2)]
        old_sb = [sb.tile([M, N], F32, name="old%d" % g) for g in range(G)]
        tp_rows = sb.tile([P, G * SQUARE], F32, name="tp_rows", align_bytes=64)
        tp_cols = sb.tile([P, G * SQUARE], F32, name="tp_cols", align_bytes=64)

        nc.vector.memset(tp_rows[:], 0.0)
        nc.sync.dma_start(out=x_raw[:], in_=packed_rows(x))
        nc.sync.dma_start(
            out=tp_rows[0:P:SQUARE, :].rearrange("b (g c) -> b g c", c=SQUARE),
            in_=tp.rearrange("g (b c) o -> b g (c o)", c=SQUARE),
        )
        nc.sync.dma_start(out=w2_raw[:], in_=packed_rows(w2))
        nc.sync.dma_start(out=dy_raw[0][:], in_=packed_rows(dy)[:, :, :HALF])
        nc.sync.dma_start(out=wo_raw[:], in_=packed_rows(wo))
        nc.sync.dma_start(out=dy_raw[1][:], in_=packed_rows(dy)[:, :, HALF:])
        nc.sync.dma_start(out=w1_raw[:], in_=packed_rows(w1))
        for g in range(G):
            nc.sync.dma_start(out=old_sb[g][:], in_=old[g])

        def operand(name, cols):
            return (
                sb.tile([P, cols, PACK], BF16, name=name + "_bf", align_bytes=64),
                sb.tile([P, cols], U32, name=name + "_codes", align_bytes=64),
                sb.tile([P, cols], U8, name=name + "_scales", align_bytes=64),
            )

        x_bf, x_codes, x_scales = operand("x", N)
        w2_bf, w2_codes, w2_scales = operand("w2", M)
        dy_bf, dy_codes, dy_scales = operand("dy", N)
        wo_bf, wo_codes, wo_scales = operand("wo", M)
        w1_bf, w1_codes, w1_scales = operand("w1", M)

        z_bank = [ps.tile([M, N], F32, name="z_bank%d" % g) for g in range(G)]
        c_bank = [ps.tile([M, N], F32, name="c_bank%d" % g) for g in range(G)]

        def products(banks, w_codes, w_scales, a_codes, a_scales):
            for g in range(G):
                rows = slice(ROWS * g, ROWS * (g + 1))
                nc.tensor.matmul_mx(
                    out=banks[g][:],
                    lhsT=w_codes[rows, :].bitcast(FP8X4),
                    lhsT_scale=w_scales[rows, :],
                    rhs=a_codes[rows, :].bitcast(FP8X4),
                    rhs_scale=a_scales[rows, :],
                    start=True,
                    stop=True,
                )

        th = [sb.tile([M, N], F32, name="th%d" % g) for g in range(G)]
        gate0 = sb.tile([M, N], F32, name="gate0")
        ex = [sb.tile([M, N], F32, name="ex%d" % g) for g in range(G)]
        prod = [sb.tile([M, N], F32, name="prod%d" % g) for g in range(G)]
        part = [sb.tile([M, N], F32, name="part%d" % g) for g in range(G)]
        res = [sb.tile([M, N], F32, name="res%d" % g) for g in range(G)]
        ex_sum = sb.tile([M, G], F32, name="ex_sum")
        prod_sum = sb.tile([M, G], F32, name="prod_sum")
        inv_ex_sum = sb.tile([M, G], F32, name="inv_ex_sum")
        half_tp = sb.tile([M, G], F32, name="half_tp")
        minus_half_tp = sb.tile([M, G], F32, name="minus_half_tp")
        factor = sb.tile([M, G], F32, name="factor")
        tp_of_groups = tp_cols[:, 0 : G * SQUARE : SQUARE]

        def tanh(g):
            nc.scalar.activation(out=th[g][:], in_=z_bank[g][:], func=ACT.Tanh, scale=0.5)

        round_and_interleave(nc.vector.tensor_copy, x_bf[:, :X_VECTOR_COLS, :], x_raw[:, :, :X_VECTOR_COLS])
        round_and_interleave(nc.scalar.copy, x_bf[:, X_VECTOR_COLS:, :], x_raw[:, :, X_VECTOR_COLS:])
        round_and_interleave(nc.scalar.copy, w2_bf[:], w2_raw[:])
        nc.vector.transpose(out=tp_cols[:], in_=tp_rows[:])
        quantize(nc, x_codes[:], x_scales[:], x_bf[:])
        quantize(nc, w2_codes[:], w2_scales[:], w2_bf[:])
        nc.vector.tensor_scalar(out=half_tp[:], in0=tp_of_groups, scalar1=0.5, scalar2=None, op0=ALU.mult)
        products(z_bank, w2_codes, w2_scales, x_codes, x_scales)

        round_and_interleave(nc.vector.tensor_copy, dy_bf[:, :HALF, :], dy_raw[0][:])
        round_and_interleave(nc.scalar.copy, wo_bf[:], wo_raw[:])
        quantize(nc, dy_codes[:, :HALF], dy_scales[:, :HALF], dy_bf[:, :HALF, :])
        quantize(nc, wo_codes[:], wo_scales[:], wo_bf[:])
        tanh(0)
        cut = HALF + DY_VECTOR_COLS
        round_and_interleave(nc.vector.tensor_copy, dy_bf[:, HALF:cut, :], dy_raw[1][:, :, :DY_VECTOR_COLS])
        round_and_interleave(nc.scalar.copy, dy_bf[:, cut:, :], dy_raw[1][:, :, DY_VECTOR_COLS:])
        quantize(nc, dy_codes[:, HALF:], dy_scales[:, HALF:], dy_bf[:, HALF:, :])
        products(c_bank, wo_codes, wo_scales, dy_codes, dy_scales)

        nc.scalar.activation(
            out=gate0[:], in_=th[0][:], func=ACT.Identity, scale=half_tp[:, 0:1], bias=half_tp[:, 0:1]
        )
        for g in range(1, G):
            tanh(g)

        round_and_interleave(nc.vector.tensor_copy, w1_bf[:], w1_raw[:])
        nc.vector.tensor_scalar(out=minus_half_tp[:], in0=tp_of_groups, scalar1=-0.5, scalar2=None, op0=ALU.mult)
        quantize(nc, w1_codes[:], w1_scales[:], w1_bf[:])
        products(z_bank, w1_codes, w1_scales, x_codes, x_scales)
        for g in range(G):
            nc.scalar.activation(
                out=ex[g][:],
                in_=z_bank[g][:],
                func=ACT.Exp,
                scale=tp_cols[:, SQUARE * g : SQUARE * g + 1],
                accum_out=ex_sum[:, g : g + 1],
            )

        def product_with_c0(g):
            nc.vector.scalar_tensor_tensor(
                out=prod[g][:],
                in0=gate0[:] if g == 0 else th[g][:],
                scalar=0.0 if g == 0 else 1.0,
                in1=c_bank[g][:],
                op0=ALU.add,
                op1=ALU.mult,
                accum_out=prod_sum[:, g : g + 1],
            )

        def add_old(g, cols):
            nc.vector.scalar_tensor_tensor(
                out=part[g][:, cols],
                in0=prod[g][:, cols],
                scalar=half_tp[:, g : g + 1],
                in1=old_sb[g][:, cols],
                op0=ALU.mult,
                op1=ALU.add,
            )

        def invert_sums(groups):
            nc.vector.reciprocal(out=inv_ex_sum[:, groups], in_=ex_sum[:, groups])

        def row_factor(g):
            nc.vector.tensor_scalar(
                out=factor[:, g : g + 1],
                in0=prod_sum[:, g : g + 1],
                scalar1=inv_ex_sum[:, g : g + 1],
                scalar2=-1.0 if g == 0 else minus_half_tp[:, g : g + 1],
                op0=ALU.mult,
                op1=ALU.mult,
            )

        def finish(g, cols):
            nc.vector.scalar_tensor_tensor(
                out=res[g][:, cols],
                in0=ex[g][:, cols],
                scalar=factor[:, g : g + 1],
                in1=part[g][:, cols],
                op0=ALU.mult,
                op1=ALU.add,
            )
            nc.sync.dma_start(out=out[g][:, cols], in_=res[g][:, cols])

        product_with_c0(0)
        nc.gpsimd.tensor_tensor(out=part[0][:], in0=prod[0][:], in1=old_sb[0][:], op=ALU.add)
        for g in range(1, G):
            product_with_c0(g)

        whole, left, right = slice(0, N), slice(0, HALF), slice(HALF, N)
        invert_sums(slice(0, 2))
        add_old(1, whole)
        row_factor(0)
        row_factor(1)
        add_old(2, whole)
        finish(0, whole)
        invert_sums(slice(2, 4))
        finish(1, whole)
        row_factor(2)
        row_factor(3)
        add_old(3, left)
        finish(2, whole)
        add_old(3, right)
        finish(3, left)
        finish(3, right)
